import numpy as np
import ml_dtypes


def mxq(x, axis, fmt="e4m3"):
    dtype, down = {"e4m3": (ml_dtypes.float8_e4m3fn, 7), "e5m2": (ml_dtypes.float8_e5m2, 14)}[fmt]
    v = np.moveaxis(np.asarray(x, np.float32).astype(ml_dtypes.bfloat16).astype(np.float64), axis, -1)
    blocks = v.reshape(v.shape[:-1] + (-1, 32))
    amax = np.abs(blocks).max(-1, keepdims=True)
    byte = np.maximum(np.where(amax > 0, np.frexp(amax)[1] - 1 + 127, 0) - down, 1)
    scale = np.exp2(byte - 127.0)
    codes = (blocks / scale).astype(np.float32).astype(dtype).astype(np.float64)
    return np.moveaxis((codes * scale).reshape(v.shape), -1, axis)


WIDE = False


def mx_kscale(k):
    if not WIDE:
        return np.ones(k)
    levels = np.array([10, -10, 5, -5, 0])
    if k % 512:
        return np.exp2(np.random.permutation(np.resize(levels, k // 32))).repeat(32)
    a = np.empty((k // 512, 16))
    for p in range(k // 512):
        a[p, :8] = np.random.permutation(np.resize(levels, 8))
        for g in range(8):
            far = levels[np.abs(levels - a[p, g]) >= 10]
            a[p, g + 8] = far[np.random.randint(len(far))]
    return np.exp2(a.ravel()).repeat(32)


def f64(x):
    return np.asarray(x).astype(np.float64)


def striped(idx):
    return np.tile(idx.reshape(-1, 16).T, (8, 1)).astype(np.uint16)


def unstriped(offs):
    return offs[:16].T.reshape(-1).astype(np.int64)


def pack_weight(w):
    k, n = w.shape
    w = f64(np.asarray(w, np.float32).astype(ml_dtypes.bfloat16)).reshape(k // 32, 32, n)
    amax = np.abs(w).max(1)
    byte = np.clip(np.where(amax > 0, np.frexp(amax)[1] - 1 + 127 - 7, 1), 1, 254)
    scaled = (w * np.exp2(127.0 - byte)[:, None, :]).reshape(k, n).astype(np.float32)
    words = np.ascontiguousarray(scaled.reshape(k // 512, 128, 4, n).transpose(0, 1, 3, 2)).astype(ml_dtypes.float8_e4m3fn).view(np.uint8)
    return words, np.ascontiguousarray(byte.astype(np.uint8).reshape(k // 512, 16, n))


def unpack_weight(words, scales):
    g, p, n, _ = words.shape
    vals = np.ascontiguousarray(words).view(ml_dtypes.float8_e4m3fn).astype(np.float64) * np.repeat(np.exp2(scales.astype(np.float64) - 127.0), 8, axis=1)[..., None]
    return vals.transpose(0, 1, 3, 2).reshape(g * 512, n)


K, T, S, N = 1024, 2048, 1024, 512
P = 2 ** 7


def setup_inputs():
    n = np.random.standard_normal
    s = mx_kscale(K)[:, None]
    c = mx_kscale(S)
    packed_xT = pack_weight(n((K, T)) * s)
    return {
        "x_words": packed_xT[0],
        "x_scales": packed_xT[1],
        "rot": (n((K, N)) / np.sqrt(K) / s).astype(np.float32),
        "mean": (np.tile(0.3 * n(N), (P, 1))).astype(np.float32),
        "wgt": (np.random.uniform(0.3, 1.0, (S, 1)) * c[:, None] / np.sqrt(S)).astype(np.float32),
        "inv": (np.random.uniform(0.6, 1.4, (S, 1)) / c[:, None]).astype(np.float32),
        "offs": striped(np.random.permutation(T)[:S]),
    }


def reference(x_words, x_scales, rot, mean, wgt, inv, offs):
    xq = unpack_weight(x_words, x_scales)[:, unstriped(offs)]
    rotq = mxq(f64(rot), 0, "e4m3")
    y = (xq.T @ rotq) - f64(mean)[:1]
    sg = y / (np.abs(y) + 0.05)
    a = f64(wgt) * sg
    vv = f64(inv) * y
    return mxq(a, 0, "e4m3").T @ mxq(vv, 0, "e4m3")

@@ -1,0 +1,264 @@
+from contextlib import ExitStack
+
+import concourse.mybir as mybir
+
+K, T, S, N = 1024, 2048, 1024, 512
+FLOPS = 2 * S * K * N + 2 * S * N * N
+
+F32 = mybir.dt.float32
+BF16 = mybir.dt.bfloat16
+I32 = mybir.dt.int32
+U32 = mybir.dt.uint32
+U16 = mybir.dt.uint16
+U8 = mybir.dt.uint8
+FP8X4 = mybir.dt.float8_e4m3fn_x4
+ACT = mybir.ActivationFunctionType
+ALU = mybir.AluOpType
+
+P = 128
+PACK = 4
+PASS = P * PACK
+K_PASSES = K // PASS
+T_PASSES = S // PASS
+HALF = N // 2
+RUN = 8
+SOFT = 0.05
+
+
+def tile_picked_yitq_hard_p_kernel(tc, x_words, x_scales, rot, mean, wgt, inv, offs, out):
+    nc = tc.nc
+    with ExitStack() as ctx:
+        keep = ctx.enter_context(tc.tile_pool(name="keep", bufs=1))
+        work = ctx.enter_context(tc.tile_pool(name="work", bufs=2))
+        zps = ctx.enter_context(tc.psum_pool(name="zps", bufs=4))
+        ops = ctx.enter_context(tc.psum_pool(name="ops", bufs=1))
+
+        offsets = keep.tile([P, S // 16], U16, name="offsets")
+        nc.sync.dma_start(offsets[:], offs)
+
+        scale_win = keep.tile([P, T], U8, name="scale_win", align_bytes=64)
+        nc.gpsimd.memset(scale_win[:].bitcast(I32), 0)
+        for q in range(4):
+            queue = nc.sync if q % 2 == 0 else nc.scalar
+            queue.dma_start(scale_win[32 * q : 32 * q + 4 * K_PASSES, :].bitcast(I32), x_scales[:, 4 * q : 4 * q + 4, :].bitcast(I32))
+
+        rows = keep.tile([P, T_PASSES * P], F32, name="rows", tag="floats")
+        nc.gpsimd.memset(rows[:], 0.0)
+        for i, src in enumerate((wgt, inv)):
+            nc.scalar.dma_start(
+                rows[PACK * i : PACK * (i + 1), :].rearrange("j (c r) -> j c r", r=RUN),
+                src.rearrange("(c j r) o -> j c (r o)", j=PACK, r=RUN),
+            )
+        blank = keep.tile([P, P], F32, name="blank", tag="words", align_bytes=64)
+        nc.gpsimd.memset(blank[:], 0.0)
+        ident = keep.tile([P, P], F32, name="ident")
+        nc.gpsimd.affine_select(out=ident[:], in_=blank[:], compare_op=ALU.not_equal, fill=1.0, base=0, pattern=[[-1, P]], channel_multiplier=1)
+        half = keep.tile([P, T_PASSES, PACK], F32, name="half")
+        nc.gpsimd.memset(half[:], 0.5)
+        warm = keep.tile([P, 1], F32, name="warm")
+        nc.scalar.activation(warm[:], half[:, 0, 0:1], ACT.Abs_reciprocal_sqrt)
+
+        words = keep.tile([P, K_PASSES * T], U32, name="words", tag="words", align_bytes=64)
+        word_win = [words[:, o * T : (o + 1) * T] for o in range(K_PASSES)]
+        for o in range(K_PASSES):
+            nc.sync.dma_start(word_win[o].bitcast(I32), x_words[o].rearrange("p n r -> p (n r)").bitcast(I32))
+
+        turned = ops.tile([P, T_PASSES, P], F32, name="turned", tag="out3")
+        for b in range(T_PASSES):
+            nc.tensor.transpose(turned[:, b, :], rows[:, b * P : (b + 1) * P], ident[:])
+        piece = PACK * HALF
+        floats = keep.tile([P, 2 * K_PASSES * piece + N], F32, name="floats", tag="floats")
+        mean_sb = floats[:, 2 * K_PASSES * piece :]
+        rot_raw = {}
+        for h in range(2):
+            for o in range(K_PASSES):
+                at = (h * K_PASSES + o) * piece
+                rot_raw[(o, h)] = floats[:, at : at + piece].rearrange("p (j w) -> p j w", j=PACK)
+                nc.sync.dma_start(rot_raw[(o, h)], rot[o * PASS : (o + 1) * PASS, h * HALF : (h + 1) * HALF].rearrange("(p j) w -> p j w", j=PACK))
+            if h == 0:
+                nc.sync.dma_start(mean_sb, mean)
+        fac = keep.tile([P, T_PASSES, 2 * PACK], F32, name="fac")
+        nc.scalar.copy(fac[:], turned[:, :, 0 : 2 * PACK])
+        two = keep.tile([P, T_PASSES, PACK], F32, name="two")
+        sgn = keep.tile([P, T_PASSES, PACK], F32, name="sgn")
+        absw = keep.tile([P, T_PASSES, PACK], F32, name="absw")
+        rootw = keep.tile([P, T_PASSES, PACK], F32, name="rootw")
+        invs = keep.tile([P, T_PASSES, PACK], F32, name="invs")
+        nc.gpsimd.tensor_scalar(two[:], fac[:, :, 0:PACK], 0.0, 2.0, ALU.is_ge, ALU.mult)
+        nc.gpsimd.tensor_scalar(sgn[:], two[:], 1.0, -1.0, ALU.mult, ALU.add)
+        nc.gpsimd.tensor_tensor(absw[:], fac[:, :, 0:PACK], sgn[:], ALU.mult)
+        nc.gpsimd.tensor_tensor(invs[:], fac[:, :, PACK : 2 * PACK], sgn[:], ALU.mult)
+        nc.gpsimd.tensor_tensor(rootw[:], absw[:], half[:], ALU.pow)
+
+        cols = PASS // 16
+        x_codes = {}
+
+        def gather_words(o, b):
+            picked = keep.tile([P, PASS], U32, name="x_codes%d%d" % (o, b), align_bytes=64)
+            nc.vector.tensor_copy(
+                picked[:].rearrange("p (j g r) -> p g j r", j=PACK, r=RUN),
+                word_win[o].indirect(offsets[:, b * cols : (b + 1) * cols]),
+            )
+            x_codes[(o, b)] = picked
+
+        listed = keep.tile([P, S], U8, name="listed", align_bytes=64)
+        nc.vector.tensor_copy(listed[:], scale_win[:].indirect(offsets[:]))
+        gather_words(0, 0)
+        x_sc = keep.tile([P, S], U8, name="x_sc", align_bytes=64)
+        nc.vector.tensor_copy(
+            x_sc[:].bitcast(I32).rearrange("p (b j g r) -> p b g j r", b=T_PASSES, j=PACK, r=RUN // 4),
+            listed[:].bitcast(I32).rearrange("p (b g j r) -> p b g j r", b=T_PASSES, j=PACK, r=RUN // 4),
+        )
+        gather_words(0, 1)
+        gather_words(1, 0)
+
+        rot_codes, rot_sc = {}, {}
+
+        def weave_rot(o, h):
+            woven = keep.tile([P, HALF * PACK], BF16, name="rot_woven%d%d" % (o, h), align_bytes=64)
+            nc.scalar.copy(
+                woven[:].rearrange("p (c i j) -> p c j i", i=4, j=PACK),
+                rot_raw[(o, h)].rearrange("p j (c i) -> p c j i", i=4),
+            )
+            return woven
+
+        def quant_rot(o, h, woven):
+            codes = keep.tile([P, HALF], U32, name="rot_codes%d%d" % (o, h), align_bytes=64)
+            sc = keep.tile([P, HALF], U8, name="rot_sc%d%d" % (o, h), align_bytes=64)
+            nc.vector.quantize_mx(out=codes[:].bitcast(FP8X4), scales=sc[:], in_=woven[:])
+            rot_codes[(o, h)] = codes
+            rot_sc[(o, h)] = sc
+
+        woven0 = [weave_rot(o, 0) for o in range(K_PASSES)]
+        for o in range(K_PASSES):
+            quant_rot(o, 0, woven0[o])
+        gather_words(1, 1)
+        woven1 = [weave_rot(o, 1) for o in range(K_PASSES)]
+
+        v_codes = [keep.tile([P, N], U32, name="v_codes%d" % b, align_bytes=64) for b in range(T_PASSES)]
+        v_sc = [keep.tile([P, N], U8, name="v_sc%d" % b, align_bytes=64) for b in range(T_PASSES)]
+        a_codes, a_sc, ys, ss = {}, {}, {}, {}
+
+        def centre(b, h):
+            y = keep.tile([P, PACK, HALF], F32, name="y%d%d" % (b, h))
+            for jj in range(2):
+                z = zps.tile([P, 2, HALF], F32, name="z")
+                for e in range(2):
+                    c0 = (2 * jj + e) * P
+                    for o in range(K_PASSES):
+                        nc.tensor.matmul_mx(
+                            out=z[:, e, :],
+                            lhsT=x_codes[(o, b)][:, c0 : c0 + P].bitcast(FP8X4),
+                            lhsT_scale=x_sc[4 * o : P, b * PASS + c0 : b * PASS + c0 + P],
+                            rhs=rot_codes[(o, h)][:].bitcast(FP8X4),
+                            rhs_scale=rot_sc[(o, h)][:],
+                            start=(o == 0),
+                            stop=(o == K_PASSES - 1),
+                        )
+                nc.vector.tensor_tensor(
+                    y[:, 2 * jj : 2 * jj + 2, :],
+                    z[:],
+                    mean_sb[:, h * HALF : (h + 1) * HALF].unsqueeze(1).to_broadcast([P, 2, HALF]),
+                    ALU.subtract,
+                )
+            ys[(b, h)] = y
+
+        def soften(b, h):
+            y = ys[(b, h)]
+            u = work.tile([P, PACK, HALF], F32, name="u")
+            nc.scalar.activation(u[:], y[:], ACT.Abs)
+            r = work.tile([P, PACK, HALF], F32, name="r")
+            nc.scalar.activation(r[:], u[:], ACT.Abs_reciprocal_sqrt, bias=SOFT)
+            s = keep.tile([P, PACK, HALF], F32, name="s%d%d" % (b, h))
+            for j in range(PACK):
+                nc.scalar.activation(s[:, j, :], r[:, j, :], ACT.Square, scale=rootw[:, b, j : j + 1])
+            ss[(b, h)] = s
+
+        def make_v(b, h):
+            vv = work.tile([P, HALF * PACK], BF16, name="vv", align_bytes=64)
+            nc.vector.tensor_tensor(
+                vv[:].rearrange("p (c i j) -> p c j i", i=4, j=PACK),
+                ys[(b, h)][:].rearrange("p j (c i) -> p c j i", i=4),
+                invs[:, b, :].unsqueeze(1).unsqueeze(3).to_broadcast([P, HALF // 4, PACK, 4]),
+                ALU.mult,
+            )
+            return vv
+
+        def quant_v(b, h, vv):
+            cs = slice(h * HALF, (h + 1) * HALF)
+            nc.vector.quantize_mx(out=v_codes[b][:, cs].bitcast(FP8X4), scales=v_sc[b][:, cs], in_=vv[:])
+
+        def make_a(b, h):
+            a = work.tile([P, HALF * PACK], BF16, name="a", align_bytes=64)
+            nc.vector.tensor_tensor(
+                a[:].rearrange("p (c i j) -> p c j i", i=4, j=PACK),
+                ys[(b, h)][:].rearrange("p j (c i) -> p c j i", i=4),
+                ss[(b, h)][:].rearrange("p j (c i) -> p c j i", i=4),
+                ALU.mult,
+            )
+            return a
+
+        def quant_a(b, h, a):
+            codes = keep.tile([P, HALF], U32, name="a_codes%d%d" % (b, h), align_bytes=64)
+            sc = keep.tile([P, HALF], U8, name="a_sc%d%d" % (b, h), align_bytes=64)
+            nc.vector.quantize_mx(out=codes[:].bitcast(FP8X4), scales=sc[:], in_=a[:])
+            a_codes[(b, h)] = codes
+            a_sc[(b, h)] = sc
+
+        acc = [ops.tile([P, N], F32, name="acc%d" % i, tag="out%d" % i) for i in range(N // P)]
+
+        def outer(b, h):
+            for q in range(2):
+                i = 2 * h + q
+                nc.tensor.matmul_mx(
+                    out=acc[i][:],
+                    lhsT=a_codes[(b, h)][:, q * P : (q + 1) * P].bitcast(FP8X4),
+                    lhsT_scale=a_sc[(b, h)][:, q * P : (q + 1) * P],
+                    rhs=v_codes[b][:].bitcast(FP8X4),
+                    rhs_scale=v_sc[b][:],
+                    start=(b == 0),
+                    stop=(b == T_PASSES - 1),
+                )
+
+        def store(i):
+            res = keep.tile([P, N], F32, name="res%d" % i)
+            if i % 2 == 0:
+                nc.scalar.copy(res[:], acc[i][:])
+            else:
+                nc.vector.tensor_copy(res[:], acc[i][:])
+            nc.sync.dma_start(out[i * P : (i + 1) * P, :], res[:])
+
+        centre(0, 0)
+        soften(0, 0)
+        v00 = make_v(0, 0)
+        centre(1, 0)
+        soften(1, 0)
+        quant_v(0, 0, v00)
+        for o in range(K_PASSES):
+            quant_rot(o, 1, woven1[o])
+        v10 = make_v(1, 0)
+        a00 = make_a(0, 0)
+        quant_v(1, 0, v10)
+        centre(0, 1)
+        soften(0, 1)
+        quant_a(0, 0, a00)
+        centre(1, 1)
+        soften(1, 1)
+        a10 = make_a(1, 0)
+        v01 = make_v(0, 1)
+        quant_a(1, 0, a10)
+        v11 = make_v(1, 1)
+        quant_v(0, 1, v01)
+        a01 = make_a(0, 1)
+        quant_v(1, 1, v11)
+        outer(0, 0)
+        outer(1, 0)
+        quant_a(0, 1, a01)
+        outer(0, 1)
+        store(0)
+        store(1)
+        a11 = make_a(1, 1)
+        quant_a(1, 1, a11)
+        outer(1, 1)
+        store(2)
+        store(3)

@@ -29,8 +29,8 @@ def tile_picked_yitq_hard_p_kernel(tc, x_words, x_scales, rot, mean, wgt, inv, o
     nc = tc.nc
     with ExitStack() as ctx:
         keep = ctx.enter_context(tc.tile_pool(name="keep", bufs=1))
-        work = ctx.enter_context(tc.tile_pool(name="work", bufs=2))
-        zps = ctx.enter_context(tc.psum_pool(name="zps", bufs=4))
+        work = ctx.enter_context(tc.tile_pool(name="work", bufs=3))
+        stage = ctx.enter_context(tc.tile_pool(name="stage", bufs=1))
         ops = ctx.enter_context(tc.psum_pool(name="ops", bufs=1))
 
         offsets = keep.tile([P, S // 16], U16, name="offsets")
@@ -42,41 +42,45 @@ def tile_picked_yitq_hard_p_kernel(tc, x_words, x_scales, rot, mean, wgt, inv, o
             queue = nc.sync if q % 2 == 0 else nc.scalar
             queue.dma_start(scale_win[32 * q : 32 * q + 4 * K_PASSES, :].bitcast(I32), x_scales[:, 4 * q : 4 * q + 4, :].bitcast(I32))
 
-        rows = keep.tile([P, T_PASSES * P], F32, name="rows", tag="floats")
+        piece = PACK * HALF
+        word_bytes = 4 * K_PASSES * T
+        blank = stage.tile([P, P], F32, name="blank", offset=word_bytes - 2 * P)
+        nc.gpsimd.memset(blank[:], 0.0)
+        ident = keep.tile([P, P], F32, name="ident")
+        nc.gpsimd.affine_select(out=ident[:], in_=blank[:], compare_op=ALU.not_equal, fill=1.0, base=0, pattern=[[-1, P]], channel_multiplier=1)
+        rows = keep.tile([P, T_PASSES * P], F32, name="rows")
         nc.gpsimd.memset(rows[:], 0.0)
         for i, src in enumerate((wgt, inv)):
             nc.scalar.dma_start(
                 rows[PACK * i : PACK * (i + 1), :].rearrange("j (c r) -> j c r", r=RUN),
                 src.rearrange("(c j r) o -> j c (r o)", j=PACK, r=RUN),
             )
-        blank = keep.tile([P, P], F32, name="blank", tag="words", align_bytes=64)
-        nc.gpsimd.memset(blank[:], 0.0)
-        ident = keep.tile([P, P], F32, name="ident")
-        nc.gpsimd.affine_select(out=ident[:], in_=blank[:], compare_op=ALU.not_equal, fill=1.0, base=0, pattern=[[-1, P]], channel_multiplier=1)
         half = keep.tile([P, T_PASSES, PACK], F32, name="half")
         nc.gpsimd.memset(half[:], 0.5)
         warm = keep.tile([P, 1], F32, name="warm")
         nc.scalar.activation(warm[:], half[:, 0, 0:1], ACT.Abs_reciprocal_sqrt)
 
-        words = keep.tile([P, K_PASSES * T], U32, name="words", tag="words", align_bytes=64)
+        words = stage.tile([P, K_PASSES * T], U32, name="words", offset=0)
         word_win = [words[:, o * T : (o + 1) * T] for o in range(K_PASSES)]
-        for o in range(K_PASSES):
-            nc.sync.dma_start(word_win[o].bitcast(I32), x_words[o].rearrange("p n r -> p (n r)").bitcast(I32))
-
-        turned = ops.tile([P, T_PASSES, P], F32, name="turned", tag="out3")
-        for b in range(T_PASSES):
-            nc.tensor.transpose(turned[:, b, :], rows[:, b * P : (b + 1) * P], ident[:])
-        piece = PACK * HALF
-        floats = keep.tile([P, 2 * K_PASSES * piece + N], F32, name="floats", tag="floats")
+        floats = stage.tile([P, 2 * K_PASSES * piece + N], F32, name="floats", offset=word_bytes)
         mean_sb = floats[:, 2 * K_PASSES * piece :]
         rot_raw = {}
-        for h in range(2):
-            for o in range(K_PASSES):
-                at = (h * K_PASSES + o) * piece
-                rot_raw[(o, h)] = floats[:, at : at + piece].rearrange("p (j w) -> p j w", j=PACK)
-                nc.sync.dma_start(rot_raw[(o, h)], rot[o * PASS : (o + 1) * PASS, h * HALF : (h + 1) * HALF].rearrange("(p j) w -> p j w", j=PACK))
-            if h == 0:
-                nc.sync.dma_start(mean_sb, mean)
+
+        def load_rot(o, h):
+            at = (h * K_PASSES + o) * piece
+            rot_raw[(o, h)] = floats[:, at : at + piece].rearrange("p (j w) -> p j w", j=PACK)
+            nc.sync.dma_start(rot_raw[(o, h)], rot[o * PASS : (o + 1) * PASS, h * HALF : (h + 1) * HALF].rearrange("(p j) w -> p j w", j=PACK))
+
+        for o in range(K_PASSES):
+            nc.sync.dma_start(word_win[o].bitcast(I32), x_words[o].rearrange("p n r -> p (n r)").bitcast(I32))
+            load_rot(o, 0)
+        nc.sync.dma_start(mean_sb, mean)
+        for o in range(K_PASSES):
+            load_rot(o, 1)
+
+        turned = ops.tile([P, T_PASSES, P], F32, name="turned", tag="bank7")
+        for b in range(T_PASSES):
+            nc.tensor.transpose(turned[:, b, :], rows[:, b * P : (b + 1) * P], ident[:])
         fac = keep.tile([P, T_PASSES, 2 * PACK], F32, name="fac")
         nc.scalar.copy(fac[:], turned[:, :, 0 : 2 * PACK])
         two = keep.tile([P, T_PASSES, PACK], F32, name="two")
@@ -94,7 +98,7 @@ def tile_picked_yitq_hard_p_kernel(tc, x_words, x_scales, rot, mean, wgt, inv, o
         x_codes = {}
 
         def gather_words(o, b):
-            picked = keep.tile([P, PASS], U32, name="x_codes%d%d" % (o, b), align_bytes=64)
+            picked = keep.tile([P, PASS], U32, name="x_codes", tag="codes%d%d" % (o, b), align_bytes=64)
             nc.vector.tensor_copy(
                 picked[:].rearrange("p (j g r) -> p g j r", j=PACK, r=RUN),
                 word_win[o].indirect(offsets[:, b * cols : (b + 1) * cols]),
@@ -110,17 +114,20 @@ def tile_picked_yitq_hard_p_kernel(tc, x_words, x_scales, rot, mean, wgt, inv, o
             listed[:].bitcast(I32).rearrange("p (b g j r) -> p b g j r", b=T_PASSES, j=PACK, r=RUN // 4),
         )
         gather_words(0, 1)
-        gather_words(1, 0)
 
         rot_codes, rot_sc = {}, {}
 
-        def weave_rot(o, h):
-            woven = keep.tile([P, HALF * PACK], BF16, name="rot_woven%d%d" % (o, h), align_bytes=64)
-            nc.scalar.copy(
-                woven[:].rearrange("p (c i j) -> p c j i", i=4, j=PACK),
-                rot_raw[(o, h)].rearrange("p j (c i) -> p c j i", i=4),
-            )
+        def weave_rot(o, h, shares):
+            woven = keep.tile([P, HALF * PACK], BF16, name="rot_woven", tag="codes11" if (o, h) == (1, 0) else "woven%d%d" % (o, h), align_bytes=64)
+            for copy, c0, c1 in shares:
+                copy(
+                    woven[:, c0 * PACK : c1 * PACK].rearrange("p (c i j) -> p c j i", i=4, j=PACK),
+                    rot_raw[(o, h)][:, :, c0:c1].rearrange("p j (c i) -> p c j i", i=4),
+                )
             return woven
+
+        on_scalar = [(nc.scalar.copy, 0, HALF)]
+        shared = [(nc.scalar.copy, 0, 96), (nc.vector.tensor_copy, 96, HALF)]
 
         def quant_rot(o, h, woven):
             codes = keep.tile([P, HALF], U32, name="rot_codes%d%d" % (o, h), align_bytes=64)
@@ -129,136 +136,179 @@ def tile_picked_yitq_hard_p_kernel(tc, x_words, x_scales, rot, mean, wgt, inv, o
             rot_codes[(o, h)] = codes
             rot_sc[(o, h)] = sc
 
-        woven0 = [weave_rot(o, 0) for o in range(K_PASSES)]
-        for o in range(K_PASSES):
-            quant_rot(o, 0, woven0[o])
+        quant_rot(0, 0, weave_rot(0, 0, on_scalar))
+        gather_words(1, 0)
+        quant_rot(1, 0, weave_rot(1, 0, shared))
         gather_words(1, 1)
-        woven1 = [weave_rot(o, 1) for o in range(K_PASSES)]
 
         v_codes = [keep.tile([P, N], U32, name="v_codes%d" % b, align_bytes=64) for b in range(T_PASSES)]
         v_sc = [keep.tile([P, N], U8, name="v_sc%d" % b, align_bytes=64) for b in range(T_PASSES)]
-        a_codes, a_sc, ys, ss = {}, {}, {}, {}
+        ys, ss, us, rs = {}, {}, {}, {}
 
-        def centre(b, h):
-            y = keep.tile([P, PACK, HALF], F32, name="y%d%d" % (b, h))
+        def product(z, b, h, j, o):
+            nc.tensor.matmul_mx(
+                out=z,
+                lhsT=x_codes[(o, b)][:, j * P : (j + 1) * P].bitcast(FP8X4),
+                lhsT_scale=x_sc[4 * o : P, b * PASS + j * P : b * PASS + (j + 1) * P],
+                rhs=rot_codes[(o, h)][:].bitcast(FP8X4),
+                rhs_scale=rot_sc[(o, h)][:],
+                start=(o == 0),
+                stop=(o == K_PASSES - 1),
+            )
+
+        for b in range(T_PASSES):
+            for h in range(2):
+                ys[(b, h)] = keep.tile([P, PACK, HALF], F32, name="y%d%d" % (b, h))
+                ss[(b, h)] = keep.tile([P, PACK, HALF], F32, name="s%d%d" % (b, h))
+                us[(b, h)] = keep.tile([P, PACK, HALF], F32, name="u%d%d" % (b, h))
+                rs[(b, h)] = keep.tile([P, PACK, HALF], F32, name="r%d%d" % (b, h))
+
+        first = {}
+        for b in range(T_PASSES):
+            for j in range(PACK):
+                first[(b, j)] = ops.tile([P, HALF], F32, name="z%d%d" % (b, j), tag="bank%d" % (PACK * b + j))
+        for o in range(K_PASSES):
+            for b in range(T_PASSES):
+                for j in range(PACK):
+                    product(first[(b, j)][:], b, 0, j, o)
+
+        def centre_first(b, js):
+            for j in range(js.start, js.stop):
+                nc.vector.tensor_tensor(ys[(b, 0)][:, j, :], first[(b, j)][:], mean_sb[:, 0:HALF], ALU.subtract)
+
+        def centre(b):
             for jj in range(2):
-                z = zps.tile([P, 2, HALF], F32, name="z")
+                z = ops.tile([P, 2, HALF], F32, name="z", tag="bank%d" % (2 * b + jj))
                 for e in range(2):
-                    c0 = (2 * jj + e) * P
                     for o in range(K_PASSES):
-                        nc.tensor.matmul_mx(
-                            out=z[:, e, :],
-                            lhsT=x_codes[(o, b)][:, c0 : c0 + P].bitcast(FP8X4),
-                            lhsT_scale=x_sc[4 * o : P, b * PASS + c0 : b * PASS + c0 + P],
-                            rhs=rot_codes[(o, h)][:].bitcast(FP8X4),
-                            rhs_scale=rot_sc[(o, h)][:],
-                            start=(o == 0),
-                            stop=(o == K_PASSES - 1),
-                        )
+                        product(z[:, e, :], b, 1, 2 * jj + e, o)
                 nc.vector.tensor_tensor(
-                    y[:, 2 * jj : 2 * jj + 2, :],
+                    ys[(b, 1)][:, 2 * jj : 2 * jj + 2, :],
                     z[:],
-                    mean_sb[:, h * HALF : (h + 1) * HALF].unsqueeze(1).to_broadcast([P, 2, HALF]),
+                    mean_sb[:, HALF:N].unsqueeze(1).to_broadcast([P, 2, HALF]),
                     ALU.subtract,
                 )
-            ys[(b, h)] = y
 
-        def soften(b, h):
-            y = ys[(b, h)]
-            u = work.tile([P, PACK, HALF], F32, name="u")
-            nc.scalar.activation(u[:], y[:], ACT.Abs)
-            r = work.tile([P, PACK, HALF], F32, name="r")
-            nc.scalar.activation(r[:], u[:], ACT.Abs_reciprocal_sqrt, bias=SOFT)
-            s = keep.tile([P, PACK, HALF], F32, name="s%d%d" % (b, h))
-            for j in range(PACK):
-                nc.scalar.activation(s[:, j, :], r[:, j, :], ACT.Square, scale=rootw[:, b, j : j + 1])
-            ss[(b, h)] = s
+        def magnitude(b, h, js, cs):
+            nc.scalar.activation(us[(b, h)][:, js, cs], ys[(b, h)][:, js, cs], ACT.Abs)
 
-        def make_v(b, h):
-            vv = work.tile([P, HALF * PACK], BF16, name="vv", align_bytes=64)
-            nc.vector.tensor_tensor(
-                vv[:].rearrange("p (c i j) -> p c j i", i=4, j=PACK),
-                ys[(b, h)][:].rearrange("p j (c i) -> p c j i", i=4),
-                invs[:, b, :].unsqueeze(1).unsqueeze(3).to_broadcast([P, HALF // 4, PACK, 4]),
-                ALU.mult,
-            )
+        def inv_root(b, h, js, cs):
+            nc.scalar.activation(rs[(b, h)][:, js, cs], us[(b, h)][:, js, cs], ACT.Abs_reciprocal_sqrt, bias=SOFT)
+
+        def squares(b, h, js, cs):
+            for j in range(js.start, js.stop):
+                nc.scalar.activation(ss[(b, h)][:, j, cs], rs[(b, h)][:, j, cs], ACT.Square, scale=rootw[:, b, j : j + 1])
+
+        def make_v(b, h, engine, pieces):
+            vv = keep.tile([P, HALF * PACK], BF16, name="vv%d%d" % (b, h), align_bytes=64)
+            width = HALF // pieces
+            for c0 in range(0, HALF, width):
+                engine.tensor_tensor(
+                    vv[:, c0 * PACK : (c0 + width) * PACK].rearrange("p (c i j) -> p c j i", i=4, j=PACK),
+                    ys[(b, h)][:, :, c0 : c0 + width].rearrange("p j (c i) -> p c j i", i=4),
+                    invs[:, b, :].unsqueeze(1).unsqueeze(3).to_broadcast([P, width // 4, PACK, 4]),
+                    ALU.mult,
+                )
             return vv
 
         def quant_v(b, h, vv):
             cs = slice(h * HALF, (h + 1) * HALF)
             nc.vector.quantize_mx(out=v_codes[b][:, cs].bitcast(FP8X4), scales=v_sc[b][:, cs], in_=vv[:])
 
-        def make_a(b, h):
-            a = work.tile([P, HALF * PACK], BF16, name="a", align_bytes=64)
+        def make_a(b, h, cs):
+            a = work.tile([P, (cs.stop - cs.start) * PACK], BF16, name="a", align_bytes=64)
             nc.vector.tensor_tensor(
                 a[:].rearrange("p (c i j) -> p c j i", i=4, j=PACK),
-                ys[(b, h)][:].rearrange("p j (c i) -> p c j i", i=4),
-                ss[(b, h)][:].rearrange("p j (c i) -> p c j i", i=4),
+                ys[(b, h)][:, :, cs].rearrange("p j (c i) -> p c j i", i=4),
+                ss[(b, h)][:, :, cs].rearrange("p j (c i) -> p c j i", i=4),
                 ALU.mult,
             )
             return a
 
-        def quant_a(b, h, a):
-            codes = keep.tile([P, HALF], U32, name="a_codes%d%d" % (b, h), align_bytes=64)
-            sc = keep.tile([P, HALF], U8, name="a_sc%d%d" % (b, h), align_bytes=64)
-            nc.vector.quantize_mx(out=codes[:].bitcast(FP8X4), scales=sc[:], in_=a[:])
-            a_codes[(b, h)] = codes
-            a_sc[(b, h)] = sc
+        a_codes = [keep.tile([P, N], U32, name="a_codes%d" % b, align_bytes=64) for b in range(T_PASSES)]
+        a_sc = [keep.tile([P, N], U8, name="a_sc%d" % b, align_bytes=64) for b in range(T_PASSES)]
 
-        acc = [ops.tile([P, N], F32, name="acc%d" % i, tag="out%d" % i) for i in range(N // P)]
+        def quant_a(b, h, cs, a):
+            at = slice(h * HALF + cs.start, h * HALF + cs.stop)
+            nc.vector.quantize_mx(out=a_codes[b][:, at].bitcast(FP8X4), scales=a_sc[b][:, at], in_=a[:])
 
-        def outer(b, h):
-            for q in range(2):
-                i = 2 * h + q
-                nc.tensor.matmul_mx(
-                    out=acc[i][:],
-                    lhsT=a_codes[(b, h)][:, q * P : (q + 1) * P].bitcast(FP8X4),
-                    lhsT_scale=a_sc[(b, h)][:, q * P : (q + 1) * P],
-                    rhs=v_codes[b][:].bitcast(FP8X4),
-                    rhs_scale=v_sc[b][:],
-                    start=(b == 0),
-                    stop=(b == T_PASSES - 1),
-                )
+        def outer(b, i, dst, cs):
+            nc.tensor.matmul_mx(
+                out=dst[:],
+                lhsT=a_codes[b][:, i * P : (i + 1) * P].bitcast(FP8X4),
+                lhsT_scale=a_sc[b][:, i * P : (i + 1) * P],
+                rhs=v_codes[b][:, cs].bitcast(FP8X4),
+                rhs_scale=v_sc[b][:, cs],
+                start=(b == 0),
+                stop=(b == T_PASSES - 1),
+            )
 
-        def store(i):
-            res = keep.tile([P, N], F32, name="res%d" % i)
-            if i % 2 == 0:
-                nc.scalar.copy(res[:], acc[i][:])
-            else:
-                nc.vector.tensor_copy(res[:], acc[i][:])
-            nc.sync.dma_start(out[i * P : (i + 1) * P, :], res[:])
+        def store(i, src, cs, copy, queue):
+            res = keep.tile([P, cs.stop - cs.start], F32, name="res%d_%d" % (i, cs.start))
+            copy(res[:], src[:])
+            queue.dma_start(out[i * P : (i + 1) * P, cs], res[:])
 
-        centre(0, 0)
-        soften(0, 0)
-        v00 = make_v(0, 0)
-        centre(1, 0)
-        soften(1, 0)
+        allj, allc = slice(0, PACK), slice(0, HALF)
+        lo, hi = slice(0, P), slice(P, HALF)
+        ja, jb = slice(0, 2), slice(2, 4)
+        woven01 = weave_rot(0, 1, on_scalar)
+        woven11 = weave_rot(1, 1, on_scalar)
+        centre_first(0, ja)
+        magnitude(0, 0, ja, allc)
+        centre_first(0, jb)
+        magnitude(0, 0, jb, allc)
+        inv_root(0, 0, ja, allc)
+        inv_root(0, 0, jb, allc)
+        quant_rot(0, 1, woven01)
+        centre_first(1, ja)
+        quant_rot(1, 1, woven11)
+        centre_first(1, jb)
+        squares(0, 0, allj, allc)
+        magnitude(1, 0, allj, allc)
+        v00 = make_v(0, 0, nc.vector, 1)
+        centre(0)
         quant_v(0, 0, v00)
-        for o in range(K_PASSES):
-            quant_rot(o, 1, woven1[o])
-        v10 = make_v(1, 0)
-        a00 = make_a(0, 0)
+        centre(1)
+        v10 = make_v(1, 0, nc.vector, 1)
+        inv_root(1, 0, allj, allc)
+        magnitude(0, 1, allj, allc)
+        squares(1, 0, allj, allc)
+        inv_root(0, 1, allj, allc)
+        magnitude(1, 1, allj, allc)
+        squares(0, 1, allj, allc)
+        inv_root(1, 1, allj, lo)
+        inv_root(1, 1, allj, hi)
+        squares(1, 1, allj, lo)
+        squares(1, 1, allj, hi)
+        a00 = make_a(0, 0, allc)
         quant_v(1, 0, v10)
-        centre(0, 1)
-        soften(0, 1)
-        quant_a(0, 0, a00)
-        centre(1, 1)
-        soften(1, 1)
-        a10 = make_a(1, 0)
-        v01 = make_v(0, 1)
-        quant_a(1, 0, a10)
-        v11 = make_v(1, 1)
+        v01 = make_v(0, 1, nc.vector, 1)
+        quant_a(0, 0, allc, a00)
+        v11 = make_v(1, 1, nc.vector, 1)
         quant_v(0, 1, v01)
-        a01 = make_a(0, 1)
+        a10 = make_a(1, 0, allc)
         quant_v(1, 1, v11)
-        outer(0, 0)
-        outer(1, 0)
-        quant_a(0, 1, a01)
-        outer(0, 1)
-        store(0)
-        store(1)
-        a11 = make_a(1, 1)
-        quant_a(1, 1, a11)
-        outer(1, 1)
-        store(2)
-        store(3)
+        a01 = make_a(0, 1, allc)
+        quant_a(1, 0, allc, a10)
+        whole, left, right = slice(0, N), slice(0, HALF), slice(HALF, N)
+        acc = [ops.tile([P, N], F32, name="acc%d" % i, tag="bank%d" % (PACK + i)) for i in range(3)]
+        last = [ops.tile([P, HALF], F32, name="last%d" % i, tag="bank%d" % (7 * (1 - i))) for i in range(2)]
+        for i in range(2):
+            outer(0, i, acc[i], whole)
+            outer(1, i, acc[i], whole)
+        a_lo = make_a(1, 1, lo)
+        quant_a(0, 1, allc, a01)
+        outer(0, 2, acc[2], whole)
+        outer(0, 3, last[0], left)
+        outer(0, 3, last[1], right)
+        store(0, acc[0], whole, nc.scalar.copy, nc.sync)
+        store(1, acc[1], whole, nc.scalar.copy, nc.sync)
+        quant_a(1, 1, lo, a_lo)
+        outer(1, 2, acc[2], whole)
+        a_hi = make_a(1, 1, hi)
+        quant_a(1, 1, hi, a_hi)
+        outer(1, 3, last[0], left)
+        outer(1, 3, last[1], right)
+        store(2, acc[2], whole, nc.scalar.copy, nc.sync)
+        store(3, last[0], left, nc.vector.tensor_copy, nc.sync)
+        store(3, last[1], right, nc.vector.tensor_copy, nc.sync)

@@ -23,6 +23,7 @@ T_PASSES = S // PASS
 HALF = N // 2
 RUN = 8
 SOFT = 0.05
+TINY = 2.0**-126
 
 
 def tile_picked_yitq_hard_p_kernel(tc, x_words, x_scales, rot, mean, wgt, inv, offs, out):
@@ -36,6 +37,10 @@ def tile_picked_yitq_hard_p_kernel(tc, x_words, x_scales, rot, mean, wgt, inv, o
         offsets = keep.tile([P, S // 16], U16, name="offsets")
         nc.sync.dma_start(offsets[:], offs)
 
+        listed_rows = keep.tile([2 * T_PASSES, PASS], F32, name="listed_rows")
+        for i, src in enumerate((wgt, inv)):
+            nc.scalar.dma_start(listed_rows[T_PASSES * i : T_PASSES * (i + 1), :], src.rearrange("(b t) o -> b (t o)", b=T_PASSES))
+
         scale_win = keep.tile([P, T], U8, name="scale_win", align_bytes=64)
         nc.gpsimd.memset(scale_win[:].bitcast(I32), 0)
         for q in range(4):
@@ -48,17 +53,12 @@ def tile_picked_yitq_hard_p_kernel(tc, x_words, x_scales, rot, mean, wgt, inv, o
         nc.gpsimd.memset(blank[:], 0.0)
         ident = keep.tile([P, P], F32, name="ident")
         nc.gpsimd.affine_select(out=ident[:], in_=blank[:], compare_op=ALU.not_equal, fill=1.0, base=0, pattern=[[-1, P]], channel_multiplier=1)
-        rows = keep.tile([P, T_PASSES * P], F32, name="rows")
-        nc.gpsimd.memset(rows[:], 0.0)
-        for i, src in enumerate((wgt, inv)):
-            nc.scalar.dma_start(
-                rows[PACK * i : PACK * (i + 1), :].rearrange("j (c r) -> j c r", r=RUN),
-                src.rearrange("(c j r) o -> j c (r o)", j=PACK, r=RUN),
-            )
-        half = keep.tile([P, T_PASSES, PACK], F32, name="half")
-        nc.gpsimd.memset(half[:], 0.5)
-        warm = keep.tile([P, 1], F32, name="warm")
-        nc.scalar.activation(warm[:], half[:, 0, 0:1], ACT.Abs_reciprocal_sqrt)
+        rows = keep.tile([P, PASS], F32, name="rows")
+        nc.scalar.activation(rows[:], ident[:, 0:1].to_broadcast([P, PASS]), ACT.Abs_reciprocal_sqrt, bias=1.0)
+        nc.scalar.copy(
+            rows[0 : 2 * T_PASSES, :].rearrange("a (j g r) -> a g j r", j=PACK, r=RUN),
+            listed_rows[:].rearrange("a (g j r) -> a g j r", j=PACK, r=RUN),
+        )
 
         words = stage.tile([P, K_PASSES * T], U32, name="words", offset=0)
         word_win = [words[:, o * T : (o + 1) * T] for o in range(K_PASSES)]
@@ -78,21 +78,24 @@ def tile_picked_yitq_hard_p_kernel(tc, x_words, x_scales, rot, mean, wgt, inv, o
         for o in range(K_PASSES):
             load_rot(o, 1)
 
-        turned = ops.tile([P, T_PASSES, P], F32, name="turned", tag="bank7")
-        for b in range(T_PASSES):
-            nc.tensor.transpose(turned[:, b, :], rows[:, b * P : (b + 1) * P], ident[:])
-        fac = keep.tile([P, T_PASSES, 2 * PACK], F32, name="fac")
-        nc.scalar.copy(fac[:], turned[:, :, 0 : 2 * PACK])
-        two = keep.tile([P, T_PASSES, PACK], F32, name="two")
-        sgn = keep.tile([P, T_PASSES, PACK], F32, name="sgn")
-        absw = keep.tile([P, T_PASSES, PACK], F32, name="absw")
-        rootw = keep.tile([P, T_PASSES, PACK], F32, name="rootw")
-        invs = keep.tile([P, T_PASSES, PACK], F32, name="invs")
-        nc.gpsimd.tensor_scalar(two[:], fac[:, :, 0:PACK], 0.0, 2.0, ALU.is_ge, ALU.mult)
+        turned = ops.tile([P, PACK, P], F32, name="turned", tag="bank7")
+        for j in range(PACK):
+            nc.tensor.transpose(turned[:, j, :], rows[:, j * P : (j + 1) * P], ident[:])
+        fac = keep.tile([P, 2 * T_PASSES, PACK], F32, name="fac")
+        nc.scalar.copy(fac[:], turned[:, :, 0 : 2 * T_PASSES].rearrange("p j a -> p a j"))
+        w_fac, inv_fac = fac[:, 0:T_PASSES, :], fac[:, T_PASSES:, :]
+        small = [P, T_PASSES, PACK]
+        two = keep.tile(small, F32, name="two")
+        sgn = keep.tile(small, F32, name="sgn")
+        absw = keep.tile(small, F32, name="absw")
+        safe = keep.tile(small, F32, name="safe")
+        invs = keep.tile(small, F32, name="invs")
+        soft_w = keep.tile(small, F32, name="soft_w")
+        nc.gpsimd.tensor_scalar(two[:], w_fac, 0.0, 2.0, ALU.is_ge, ALU.mult)
         nc.gpsimd.tensor_scalar(sgn[:], two[:], 1.0, -1.0, ALU.mult, ALU.add)
-        nc.gpsimd.tensor_tensor(absw[:], fac[:, :, 0:PACK], sgn[:], ALU.mult)
-        nc.gpsimd.tensor_tensor(invs[:], fac[:, :, PACK : 2 * PACK], sgn[:], ALU.mult)
-        nc.gpsimd.tensor_tensor(rootw[:], absw[:], half[:], ALU.pow)
+        nc.gpsimd.tensor_tensor(absw[:], w_fac, sgn[:], ALU.mult)
+        nc.gpsimd.tensor_scalar(safe[:], absw[:], TINY, 1.0, ALU.max, ALU.mult)
+        nc.gpsimd.tensor_tensor(invs[:], inv_fac, sgn[:], ALU.mult)
 
         cols = PASS // 16
         x_codes = {}
@@ -137,6 +140,9 @@ def tile_picked_yitq_hard_p_kernel(tc, x_words, x_scales, rot, mean, wgt, inv, o
             rot_sc[(o, h)] = sc
 
         quant_rot(0, 0, weave_rot(0, 0, on_scalar))
+        per_w = keep.tile(small, F32, name="per_w", tag="woven00", align_bytes=64)
+        nc.vector.reciprocal(per_w[:], safe[:])
+        nc.gpsimd.tensor_scalar(soft_w[:], per_w[:], SOFT, 0.0, ALU.mult, ALU.add)
         gather_words(1, 0)
         quant_rot(1, 0, weave_rot(1, 0, shared))
         gather_words(1, 1)
@@ -193,11 +199,14 @@ def tile_picked_yitq_hard_p_kernel(tc, x_words, x_scales, rot, mean, wgt, inv, o
             nc.scalar.activation(us[(b, h)][:, js, cs], ys[(b, h)][:, js, cs], ACT.Abs)
 
         def inv_root(b, h, js, cs):
-            nc.scalar.activation(rs[(b, h)][:, js, cs], us[(b, h)][:, js, cs], ACT.Abs_reciprocal_sqrt, bias=SOFT)
+            for j in range(js.start, js.stop):
+                nc.scalar.activation(
+                    rs[(b, h)][:, j, cs], us[(b, h)][:, j, cs], ACT.Abs_reciprocal_sqrt,
+                    bias=soft_w[:, b, j : j + 1], scale=per_w[:, b, j : j + 1],
+                )
 
         def squares(b, h, js, cs):
-            for j in range(js.start, js.stop):
-                nc.scalar.activation(ss[(b, h)][:, j, cs], rs[(b, h)][:, j, cs], ACT.Square, scale=rootw[:, b, j : j + 1])
+            nc.scalar.activation(ss[(b, h)][:, js, cs], rs[(b, h)][:, js, cs], ACT.Square)
 
         def make_v(b, h, engine, pieces):
             vv = keep.tile([P, HALF * PACK], BF16, name="vv%d%d" % (b, h), align_bytes=64)
@@ -252,7 +261,7 @@ def tile_picked_yitq_hard_p_kernel(tc, x_words, x_scales, rot, mean, wgt, inv, o
         lo, hi = slice(0, P), slice(P, HALF)
         ja, jb = slice(0, 2), slice(2, 4)
         woven01 = weave_rot(0, 1, on_scalar)
-        woven11 = weave_rot(1, 1, on_scalar)
+        woven11 = weave_rot(1, 1, shared)
         centre_first(0, ja)
         magnitude(0, 0, ja, allc)
         centre_first(0, jb)
@@ -276,8 +285,7 @@ def tile_picked_yitq_hard_p_kernel(tc, x_words, x_scales, rot, mean, wgt, inv, o
         inv_root(0, 1, allj, allc)
         magnitude(1, 1, allj, allc)
         squares(0, 1, allj, allc)
-        inv_root(1, 1, allj, lo)
-        inv_root(1, 1, allj, hi)
+        inv_root(1, 1, allj, allc)
         squares(1, 1, allj, lo)
         squares(1, 1, allj, hi)
         a00 = make_a(0, 0, allc)
@@ -311,4 +319,4 @@ def tile_picked_yitq_hard_p_kernel(tc, x_words, x_scales, rot, mean, wgt, inv, o
         outer(1, 3, last[1], right)
         store(2, acc[2], whole, nc.scalar.copy, nc.sync)
         store(3, last[0], left, nc.vector.tensor_copy, nc.sync)
-        store(3, last[1], right, nc.vector.tensor_copy, nc.sync)
+        store(3, last[1], right, nc.scalar.copy, nc.scalar)

from contextlib import ExitStack

import concourse.mybir as mybir

K, T, S, N = 1024, 2048, 1024, 512
FLOPS = 2 * S * K * N + 2 * S * N * N

F32 = mybir.dt.float32
BF16 = mybir.dt.bfloat16
I32 = mybir.dt.int32
U32 = mybir.dt.uint32
U16 = mybir.dt.uint16
U8 = mybir.dt.uint8
FP8X4 = mybir.dt.float8_e4m3fn_x4
ACT = mybir.ActivationFunctionType
ALU = mybir.AluOpType

P = 128
PACK = 4
PASS = P * PACK
K_PASSES = K // PASS
T_PASSES = S // PASS
HALF = N // 2
RUN = 8
SOFT = 0.05
TINY = 2.0**-126


def tile_picked_yitq_hard_p_kernel(tc, x_words, x_scales, rot, mean, wgt, inv, offs, out):
    nc = tc.nc
    with ExitStack() as ctx:
        keep = ctx.enter_context(tc.tile_pool(name="keep", bufs=1))
        work = ctx.enter_context(tc.tile_pool(name="work", bufs=3))
        stage = ctx.enter_context(tc.tile_pool(name="stage", bufs=1))
        ops = ctx.enter_context(tc.psum_pool(name="ops", bufs=1))

        offsets = keep.tile([P, S // 16], U16, name="offsets")
        nc.sync.dma_start(offsets[:], offs)

        listed_rows = keep.tile([2 * T_PASSES, PASS], F32, name="listed_rows")
        for i, src in enumerate((wgt, inv)):
            nc.scalar.dma_start(listed_rows[T_PASSES * i : T_PASSES * (i + 1), :], src.rearrange("(b t) o -> b (t o)", b=T_PASSES))

        scale_win = keep.tile([P, T], U8, name="scale_win", align_bytes=64)
        nc.gpsimd.memset(scale_win[:].bitcast(I32), 0)
        for q in range(4):
            queue = nc.sync if q % 2 == 0 else nc.scalar
            queue.dma_start(scale_win[32 * q : 32 * q + 4 * K_PASSES, :].bitcast(I32), x_scales[:, 4 * q : 4 * q + 4, :].bitcast(I32))

        piece = PACK * HALF
        word_bytes = 4 * K_PASSES * T
        blank = stage.tile([P, P], F32, name="blank", offset=word_bytes - 2 * P)
        nc.gpsimd.memset(blank[:], 0.0)
        ident = keep.tile([P, P], F32, name="ident")
        nc.gpsimd.affine_select(out=ident[:], in_=blank[:], compare_op=ALU.not_equal, fill=1.0, base=0, pattern=[[-1, P]], channel_multiplier=1)
        rows = keep.tile([P, PASS], F32, name="rows")
        nc.scalar.activation(rows[:], ident[:, 0:1].to_broadcast([P, PASS]), ACT.Abs_reciprocal_sqrt, bias=1.0)
        nc.scalar.copy(
            rows[0 : 2 * T_PASSES, :].rearrange("a (j g r) -> a g j r", j=PACK, r=RUN),
            listed_rows[:].rearrange("a (g j r) -> a g j r", j=PACK, r=RUN),
        )

        words = stage.tile([P, K_PASSES * T], U32, name="words", offset=0)
        word_win = [words[:, o * T : (o + 1) * T] for o in range(K_PASSES)]
        floats = stage.tile([P, 2 * K_PASSES * piece + N], F32, name="floats", offset=word_bytes)
        mean_sb = floats[:, 2 * K_PASSES * piece :]
        rot_raw = {}

        def load_rot(o, h):
            at = (h * K_PASSES + o) * piece
            rot_raw[(o, h)] = floats[:, at : at + piece].rearrange("p (j w) -> p j w", j=PACK)
            nc.sync.dma_start(rot_raw[(o, h)], rot[o * PASS : (o + 1) * PASS, h * HALF : (h + 1) * HALF].rearrange("(p j) w -> p j w", j=PACK))

        for o in range(K_PASSES):
            nc.sync.dma_start(word_win[o].bitcast(I32), x_words[o].rearrange("p n r -> p (n r)").bitcast(I32))
            load_rot(o, 0)
        nc.sync.dma_start(mean_sb, mean)
        for o in range(K_PASSES):
            load_rot(o, 1)

        turned = ops.tile([P, PACK, P], F32, name="turned", tag="bank7")
        for j in range(PACK):
            nc.tensor.transpose(turned[:, j, :], rows[:, j * P : (j + 1) * P], ident[:])
        fac = keep.tile([P, 2 * T_PASSES, PACK], F32, name="fac")
        nc.scalar.copy(fac[:], turned[:, :, 0 : 2 * T_PASSES].rearrange("p j a -> p a j"))
        w_fac, inv_fac = fac[:, 0:T_PASSES, :], fac[:, T_PASSES:, :]
        small = [P, T_PASSES, PACK]
        two = keep.tile(small, F32, name="two")
        sgn = keep.tile(small, F32, name="sgn")
        absw = keep.tile(small, F32, name="absw")
        safe = keep.tile(small, F32, name="safe")
        invs = keep.tile(small, F32, name="invs")
        soft_w = keep.tile(small, F32, name="soft_w")
        nc.gpsimd.tensor_scalar(two[:], w_fac, 0.0, 2.0, ALU.is_ge, ALU.mult)
        nc.gpsimd.tensor_scalar(sgn[:], two[:], 1.0, -1.0, ALU.mult, ALU.add)
        nc.gpsimd.tensor_tensor(absw[:], w_fac, sgn[:], ALU.mult)
        nc.gpsimd.tensor_scalar(safe[:], absw[:], TINY, 1.0, ALU.max, ALU.mult)
        nc.gpsimd.tensor_tensor(invs[:], inv_fac, sgn[:], ALU.mult)

        cols = PASS // 16
        x_codes = {}

        def gather_words(o, b):
            picked = keep.tile([P, PASS], U32, name="x_codes", tag="codes%d%d" % (o, b), align_bytes=64)
            nc.vector.tensor_copy(
                picked[:].rearrange("p (j g r) -> p g j r", j=PACK, r=RUN),
                word_win[o].indirect(offsets[:, b * cols : (b + 1) * cols]),
            )
            x_codes[(o, b)] = picked

        listed = keep.tile([P, S], U8, name="listed", align_bytes=64)
        nc.vector.tensor_copy(listed[:], scale_win[:].indirect(offsets[:]))
        gather_words(0, 0)
        x_sc = keep.tile([P, S], U8, name="x_sc", align_bytes=64)
        nc.vector.tensor_copy(
            x_sc[:].bitcast(I32).rearrange("p (b j g r) -> p b g j r", b=T_PASSES, j=PACK, r=RUN // 4),
            listed[:].bitcast(I32).rearrange("p (b g j r) -> p b g j r", b=T_PASSES, j=PACK, r=RUN // 4),
        )
        gather_words(0, 1)

        rot_codes, rot_sc = {}, {}

        def weave_rot(o, h, shares):
            woven = keep.tile([P, HALF * PACK], BF16, name="rot_woven", tag="codes11" if (o, h) == (1, 0) else "woven%d%d" % (o, h), align_bytes=64)
            for copy, c0, c1 in shares:
                copy(
                    woven[:, c0 * PACK : c1 * PACK].rearrange("p (c i j) -> p c j i", i=4, j=PACK),
                    rot_raw[(o, h)][:, :, c0:c1].rearrange("p j (c i) -> p c j i", i=4),
                )
            return woven

        on_scalar = [(nc.scalar.copy, 0, HALF)]
        shared = [(nc.scalar.copy, 0, 96), (nc.vector.tensor_copy, 96, HALF)]

        def quant_rot(o, h, woven):
            codes = keep.tile([P, HALF], U32, name="rot_codes%d%d" % (o, h), align_bytes=64)
            sc = keep.tile([P, HALF], U8, name="rot_sc%d%d" % (o, h), align_bytes=64)
            nc.vector.quantize_mx(out=codes[:].bitcast(FP8X4), scales=sc[:], in_=woven[:])
            rot_codes[(o, h)] = codes
            rot_sc[(o, h)] = sc

        quant_rot(0, 0, weave_rot(0, 0, on_scalar))
        per_w = keep.tile(small, F32, name="per_w", tag="woven00", align_bytes=64)
        nc.vector.reciprocal(per_w[:], safe[:])
        nc.gpsimd.tensor_scalar(soft_w[:], per_w[:], SOFT, 0.0, ALU.mult, ALU.add)
        gather_words(1, 0)
        quant_rot(1, 0, weave_rot(1, 0, shared))
        gather_words(1, 1)

        v_codes = [keep.tile([P, N], U32, name="v_codes%d" % b, align_bytes=64) for b in range(T_PASSES)]
        v_sc = [keep.tile([P, N], U8, name="v_sc%d" % b, align_bytes=64) for b in range(T_PASSES)]
        ys, ss, us, rs = {}, {}, {}, {}

        def product(z, b, h, j, o):
            nc.tensor.matmul_mx(
                out=z,
                lhsT=x_codes[(o, b)][:, j * P : (j + 1) * P].bitcast(FP8X4),
                lhsT_scale=x_sc[4 * o : P, b * PASS + j * P : b * PASS + (j + 1) * P],
                rhs=rot_codes[(o, h)][:].bitcast(FP8X4),
                rhs_scale=rot_sc[(o, h)][:],
                start=(o == 0),
                stop=(o == K_PASSES - 1),
            )

        for b in range(T_PASSES):
            for h in range(2):
                ys[(b, h)] = keep.tile([P, PACK, HALF], F32, name="y%d%d" % (b, h))
                ss[(b, h)] = keep.tile([P, PACK, HALF], F32, name="s%d%d" % (b, h))
                us[(b, h)] = keep.tile([P, PACK, HALF], F32, name="u%d%d" % (b, h))
                rs[(b, h)] = keep.tile([P, PACK, HALF], F32, name="r%d%d" % (b, h))

        first = {}
        for b in range(T_PASSES):
            for j in range(PACK):
                first[(b, j)] = ops.tile([P, HALF], F32, name="z%d%d" % (b, j), tag="bank%d" % (PACK * b + j))
        for o in range(K_PASSES):
            for b in range(T_PASSES):
                for j in range(PACK):
                    product(first[(b, j)][:], b, 0, j, o)

        def centre_first(b, js):
            for j in range(js.start, js.stop):
                nc.vector.tensor_tensor(ys[(b, 0)][:, j, :], first[(b, j)][:], mean_sb[:, 0:HALF], ALU.subtract)

        def centre(b):
            for jj in range(2):
                z = ops.tile([P, 2, HALF], F32, name="z", tag="bank%d" % (2 * b + jj))
                for e in range(2):
                    for o in range(K_PASSES):
                        product(z[:, e, :], b, 1, 2 * jj + e, o)
                nc.vector.tensor_tensor(
                    ys[(b, 1)][:, 2 * jj : 2 * jj + 2, :],
                    z[:],
                    mean_sb[:, HALF:N].unsqueeze(1).to_broadcast([P, 2, HALF]),
                    ALU.subtract,
                )

        def magnitude(b, h, js, cs):
            nc.scalar.activation(us[(b, h)][:, js, cs], ys[(b, h)][:, js, cs], ACT.Abs)

        def inv_root(b, h, js, cs):
            for j in range(js.start, js.stop):
                nc.scalar.activation(
                    rs[(b, h)][:, j, cs], us[(b, h)][:, j, cs], ACT.Abs_reciprocal_sqrt,
                    bias=soft_w[:, b, j : j + 1], scale=per_w[:, b, j : j + 1],
                )

        def squares(b, h, js, cs):
            nc.scalar.activation(ss[(b, h)][:, js, cs], rs[(b, h)][:, js, cs], ACT.Square)

        def make_v(b, h, engine, pieces):
            vv = keep.tile([P, HALF * PACK], BF16, name="vv%d%d" % (b, h), align_bytes=64)
            width = HALF // pieces
            for c0 in range(0, HALF, width):
                engine.tensor_tensor(
                    vv[:, c0 * PACK : (c0 + width) * PACK].rearrange("p (c i j) -> p c j i", i=4, j=PACK),
                    ys[(b, h)][:, :, c0 : c0 + width].rearrange("p j (c i) -> p c j i", i=4),
                    invs[:, b, :].unsqueeze(1).unsqueeze(3).to_broadcast([P, width // 4, PACK, 4]),
                    ALU.mult,
                )
            return vv

        def quant_v(b, h, vv):
            cs = slice(h * HALF, (h + 1) * HALF)
            nc.vector.quantize_mx(out=v_codes[b][:, cs].bitcast(FP8X4), scales=v_sc[b][:, cs], in_=vv[:])

        def make_a(b, h, cs):
            a = work.tile([P, (cs.stop - cs.start) * PACK], BF16, name="a", align_bytes=64)
            nc.vector.tensor_tensor(
                a[:].rearrange("p (c i j) -> p c j i", i=4, j=PACK),
                ys[(b, h)][:, :, cs].rearrange("p j (c i) -> p c j i", i=4),
                ss[(b, h)][:, :, cs].rearrange("p j (c i) -> p c j i", i=4),
                ALU.mult,
            )
            return a

        a_codes = [keep.tile([P, N], U32, name="a_codes%d" % b, align_bytes=64) for b in range(T_PASSES)]
        a_sc = [keep.tile([P, N], U8, name="a_sc%d" % b, align_bytes=64) for b in range(T_PASSES)]

        def quant_a(b, h, cs, a):
            at = slice(h * HALF + cs.start, h * HALF + cs.stop)
            nc.vector.quantize_mx(out=a_codes[b][:, at].bitcast(FP8X4), scales=a_sc[b][:, at], in_=a[:])

        def outer(b, i, dst, cs):
            nc.tensor.matmul_mx(
                out=dst[:],
                lhsT=a_codes[b][:, i * P : (i + 1) * P].bitcast(FP8X4),
                lhsT_scale=a_sc[b][:, i * P : (i + 1) * P],
                rhs=v_codes[b][:, cs].bitcast(FP8X4),
                rhs_scale=v_sc[b][:, cs],
                start=(b == 0),
                stop=(b == T_PASSES - 1),
            )

        def store(i, src, cs, copy, queue):
            res = keep.tile([P, cs.stop - cs.start], F32, name="res%d_%d" % (i, cs.start))
            copy(res[:], src[:])
            queue.dma_start(out[i * P : (i + 1) * P, cs], res[:])

        allj, allc = slice(0, PACK), slice(0, HALF)
        lo, hi = slice(0, P), slice(P, HALF)
        ja, jb = slice(0, 2), slice(2, 4)
        woven01 = weave_rot(0, 1, on_scalar)
        woven11 = weave_rot(1, 1, shared)
        centre_first(0, ja)
        magnitude(0, 0, ja, allc)
        centre_first(0, jb)
        magnitude(0, 0, jb, allc)
        inv_root(0, 0, ja, allc)
        inv_root(0, 0, jb, allc)
        quant_rot(0, 1, woven01)
        centre_first(1, ja)
        quant_rot(1, 1, woven11)
        centre_first(1, jb)
        squares(0, 0, allj, allc)
        magnitude(1, 0, allj, allc)
        v00 = make_v(0, 0, nc.vector, 1)
        centre(0)
        quant_v(0, 0, v00)
        centre(1)
        v10 = make_v(1, 0, nc.vector, 1)
        inv_root(1, 0, allj, allc)
        magnitude(0, 1, allj, allc)
        squares(1, 0, allj, allc)
        inv_root(0, 1, allj, allc)
        magnitude(1, 1, allj, allc)
        squares(0, 1, allj, allc)
        inv_root(1, 1, allj, allc)
        squares(1, 1, allj, lo)
        squares(1, 1, allj, hi)
        a00 = make_a(0, 0, allc)
        quant_v(1, 0, v10)
        v01 = make_v(0, 1, nc.vector, 1)
        quant_a(0, 0, allc, a00)
        v11 = make_v(1, 1, nc.vector, 1)
        quant_v(0, 1, v01)
        a10 = make_a(1, 0, allc)
        quant_v(1, 1, v11)
        a01 = make_a(0, 1, allc)
        quant_a(1, 0, allc, a10)
        whole, left, right = slice(0, N), slice(0, HALF), slice(HALF, N)
        acc = [ops.tile([P, N], F32, name="acc%d" % i, tag="bank%d" % (PACK + i)) for i in range(3)]
        last = [ops.tile([P, HALF], F32, name="last%d" % i, tag="bank%d" % (7 * (1 - i))) for i in range(2)]
        for i in range(2):
            outer(0, i, acc[i], whole)
            outer(1, i, acc[i], whole)
        a_lo = make_a(1, 1, lo)
        quant_a(0, 1, allc, a01)
        outer(0, 2, acc[2], whole)
        outer(0, 3, last[0], left)
        outer(0, 3, last[1], right)
        store(0, acc[0], whole, nc.scalar.copy, nc.sync)
        store(1, acc[1], whole, nc.scalar.copy, nc.sync)
        quant_a(1, 1, lo, a_lo)
        outer(1, 2, acc[2], whole)
        a_hi = make_a(1, 1, hi)
        quant_a(1, 1, hi, a_hi)
        outer(1, 3, last[0], left)
        outer(1, 3, last[1], right)
        store(2, acc[2], whole, nc.scalar.copy, nc.sync)
        store(3, last[0], left, nc.vector.tensor_copy, nc.sync)
        store(3, last[1], right, nc.scalar.copy, nc.scalar)
